import numpy as np
import ml_dtypes


def mxq(x, axis, fmt="e4m3"):
    dtype, down = {"e4m3": (ml_dtypes.float8_e4m3fn, 7), "e5m2": (ml_dtypes.float8_e5m2, 14)}[fmt]
    v = np.moveaxis(np.asarray(x, np.float32).astype(ml_dtypes.bfloat16).astype(np.float64), axis, -1)
    blocks = v.reshape(v.shape[:-1] + (-1, 32))
    amax = np.abs(blocks).max(-1, keepdims=True)
    byte = np.maximum(np.where(amax > 0, np.frexp(amax)[1] - 1 + 127, 0) - down, 1)
    scale = np.exp2(byte - 127.0)
    codes = (blocks / scale).astype(np.float32).astype(dtype).astype(np.float64)
    return np.moveaxis((codes * scale).reshape(v.shape), -1, axis)


WIDE = False


def mx_kscale(k):
    if not WIDE:
        return np.ones(k)
    levels = np.array([10, -10, 5, -5, 0])
    if k % 512:
        return np.exp2(np.random.permutation(np.resize(levels, k // 32))).repeat(32)
    a = np.empty((k // 512, 16))
    for p in range(k // 512):
        a[p, :8] = np.random.permutation(np.resize(levels, 8))
        for g in range(8):
            far = levels[np.abs(levels - a[p, g]) >= 10]
            a[p, g + 8] = far[np.random.randint(len(far))]
    return np.exp2(a.ravel()).repeat(32)


def f64(x):
    return np.asarray(x).astype(np.float64)


def striped(idx):
    return np.tile(idx.reshape(-1, 16).T, (8, 1)).astype(np.uint16)


def unstriped(offs):
    return offs[:16].T.reshape(-1).astype(np.int64)


E2M1 = np.array([0.0, 0.5, 1.0, 1.5, 2.0, 3.0, 4.0, 6.0, -0.0, -0.5, -1.0, -1.5, -2.0, -3.0, -4.0, -6.0])


def pack_weight(w, fmt):
    k, n = w.shape
    w = f64(np.asarray(w, np.float32).astype(ml_dtypes.bfloat16)).reshape(k // 32, 32, n)
    amax = np.abs(w).max(1)
    if fmt == "e4m3":
        byte = np.frexp(amax)[1] - 1 + 127 - 7
    else:
        mant, ex = np.frexp(amax / 6.0)
        byte = np.where(mant > 0.5, ex, ex - 1) + 127
    byte = np.clip(np.where(amax > 0, byte, 1), 1, 254)
    scaled = (w * np.exp2(127.0 - byte)[:, None, :]).reshape(k, n).astype(np.float32)
    by_word = np.ascontiguousarray(scaled.reshape(k // 512, 128, 4, n).transpose(0, 1, 3, 2))
    if fmt == "e4m3":
        words = by_word.astype(ml_dtypes.float8_e4m3fn).view(np.uint8)
    else:
        c = by_word.astype(ml_dtypes.float4_e2m1fn).view(np.uint8) & 0xF
        words = (c[..., 0::2] | (c[..., 1::2] << 4)).reshape(k // 512, 128, 2 * n)
    return np.ascontiguousarray(words), np.ascontiguousarray(byte.astype(np.uint8).reshape(k // 512, 16, n))


def unpack_weight(words, scales, fmt):
    g, _, n = scales.shape
    words = np.ascontiguousarray(words).reshape(g, 128, n, -1)
    if fmt == "e4m3":
        vals = words.view(ml_dtypes.float8_e4m3fn).astype(np.float64)
    else:
        nib = np.empty((g, 128, n, 4), np.uint8)
        nib[..., 0::2] = words & 0xF
        nib[..., 1::2] = words >> 4
        vals = E2M1[nib]
    vals = vals * np.repeat(np.exp2(scales.astype(np.float64) - 127.0), 8, axis=1)[..., None]
    return vals.transpose(0, 1, 3, 2).reshape(g * 512, n)


def gelu(v):
    return 0.5 * v * (1.0 + np.tanh(np.sqrt(2.0 / np.pi) * (v + 0.044715 * v**3)))


def striped8(idx):
    return np.concatenate([v.reshape(-1, 16).T for v in idx]).astype(np.uint16)


def unstriped8(offs):
    return np.stack([offs[16 * g:16 * g + 16].T.reshape(-1) for g in range(8)]).astype(np.int64)


def heads(h, wgt, idx8):
    r = np.arange(h.shape[0])
    return wgt[r // 4 % 128] * h[r[:, None], idx8[r % 512 // 64]]


K, H, N, T, S, T2, P = 1024, 1024, 512, 2048, 1024, 2048, 1024

def setup_inputs():
    n = np.random.standard_normal
    s = mx_kscale(K)[:, None]
    u = mx_kscale(H)[:, None]
    tab_words, tab_scales = pack_weight(n((K, T)) * s, "e4m3")
    w4_words, w4_scales = pack_weight(n((H, N)) / np.sqrt(H) / u, "e2m1")
    arms = np.stack([np.random.permutation(T2)[:P] for _ in range(8)])
    return {
        "tab_words": tab_words, "tab_scales": tab_scales,
        "offs": striped(np.random.permutation(T)[:S]),
        "w1": (n((K, H)) / np.sqrt(K) / s * u.T).astype(np.float32),
        "base": (n((H, S)) * u).astype(np.float32),
        "page0": (n((H, T2)) * u).astype(np.float32),
        "wgs": np.exp(0.3 * n((128, S))).astype(np.float32),
        "offs2": striped(np.random.permutation(T2)[:S]),
        "wgt": np.repeat(np.random.uniform(0.5, 2.0, (8, P)), 16, axis=0).astype(np.float32),
        "offs3": striped8(arms),
        "w4_words": w4_words, "w4_scales": w4_scales,
        "w2": (n((K, N)) / np.sqrt(K) / s).astype(np.float32),
        "b": n(N).astype(np.float32),
    }

def reference(tab_words, tab_scales, offs, w1, base, page0, wgs, offs2, wgt, offs3,
              w4_words, w4_scales, w2, b):
    v = unpack_weight(tab_words, tab_scales, "e4m3")[:, unstriped(offs)]
    w4 = unpack_weight(w4_words, w4_scales, "e2m1")
    w1q = mxq(f64(w1), 0, "e4m3")
    w2q = mxq(f64(w2), 0, "e4m3")
    h = np.maximum(w1q.T @ v, f64(base))
    page = f64(page0).copy()
    page[:, unstriped(offs2)] = np.tile(f64(wgs), (H // 128, 1)) * h
    x = heads(page, f64(wgt), unstriped8(offs3))
    xq = mxq(x, 0, "e4m3")
    y = w4.T @ xq
    d = w2q.T @ v
    return np.maximum(y, d) + f64(b)[:, None]

@@ -1,0 +1,261 @@
+from contextlib import ExitStack
+
+import concourse.mybir as mybir
+
+K, H, N, T, S, T2 = 1024, 1024, 512, 2048, 1024, 2048
+FLOPS = 2 * K * H * S + 2 * H * N * S + 2 * K * N * S
+
+F32 = mybir.dt.float32
+BF16 = mybir.dt.bfloat16
+I32 = mybir.dt.int32
+U32 = mybir.dt.uint32
+U16 = mybir.dt.uint16
+U8 = mybir.dt.uint8
+FP8X4 = mybir.dt.float8_e4m3fn_x4
+FP4X4 = mybir.dt.float4_e2m1fn_x4
+ALU = mybir.AluOpType
+ACT = mybir.ActivationFunctionType
+
+P = 128
+PACK = 4
+PASS = P * PACK
+PASSES = 2
+BANK = 512
+SLICES = PASSES * PACK
+CHUNK = 256
+
+
+def tile_list_rotor_fault_scores_kernel(
+    tc, tab_words, tab_scales, offs, w1, base, page0, wgs, offs2, wgt, offs3, w4_words, w4_scales, w2, b, out
+):
+    nc = tc.nc
+    with ExitStack() as ctx:
+        keep = ctx.enter_context(tc.tile_pool(name="keep", bufs=1))
+        psum = ctx.enter_context(tc.psum_pool(name="psum", bufs=1))
+
+        def bank_tile(index, shape, name):
+            return psum.tile(shape, F32, name=name, tag="bank%d" % index)
+
+        def load_list(src, name):
+            tile = keep.tile([P, S // 16], U16, name=name)
+            nc.sync.dma_start(tile[:], src)
+            return tile
+
+        def load_table_words(a):
+            tile = keep.tile([P, T], I32, name="tab_w%d" % a)
+            nc.sync.dma_start(tile[:], tab_words[a].rearrange("p t i -> p (t i)").bitcast(I32))
+            return tile
+
+        def load_weight(rows):
+            raw = keep.tile([P, PACK, PASS], F32, name="raw", tag="raw", bufs=2)
+            nc.sync.dma_start(raw[:], rows.rearrange("(p j) c -> p j c", j=PACK))
+            return raw
+
+        def bf_tile(width):
+            return keep.tile([P, width], BF16, name="bf", tag="bf", bufs=3, align_bytes=64)
+
+        def quantize(grouped, codes, scales):
+            nc.vector.quantize_mx(out=codes.bitcast(FP8X4), scales=scales, in_=grouped[:])
+
+        def quantize_weight(raw, name, dealt):
+            grouped = bf_tile(PACK * PASS)
+            if dealt:
+                nc.scalar.copy(
+                    out=grouped[:].rearrange("p (t m j) -> p m j t", t=PACK, j=PACK),
+                    in_=raw[:].rearrange("p j (m t) -> p m j t", t=PACK),
+                )
+            else:
+                nc.scalar.copy(
+                    out=grouped[:].rearrange("p (c i j) -> p c j i", i=4, j=PACK),
+                    in_=raw[:].rearrange("p j (c i) -> p c j i", i=4),
+                )
+            codes = keep.tile([P, PASS], U32, name=name + "_c", align_bytes=64)
+            scales = keep.tile([P, PASS], U8, name=name + "_s", align_bytes=64)
+            quantize(grouped, codes[:], scales[:])
+            return codes, scales
+
+        def slice_rows(src, s):
+            rows = src[PASS * (s // PACK) : PASS * (s // PACK + 1), :]
+            return rows.rearrange("(p t) j -> p t j", t=PACK)[:, s % PACK, :]
+
+        def load_base(s):
+            tile = keep.tile([P, S], F32, name="base", tag="base", bufs=4)
+            nc.sync.dma_start(tile[:], slice_rows(base, s))
+            return tile
+
+        def load_page(s):
+            tile = keep.tile([P, T2], F32, name="page", tag="page", bufs=6)
+            nc.sync.dma_start(tile[:], slice_rows(page0, s))
+            return tile
+
+        wgs_rows = wgs.rearrange("(q t) j -> q t j", t=PACK)
+
+        def load_wgs(t0, t1, name):
+            tile = keep.tile([P, t1 - t0, S], F32, name=name)
+            for quad in (0, 2, 1, 3):
+                nc.sync.dma_start(tile[32 * quad : 32 * quad + 32, :, :], wgs_rows[:, t0:t1, :])
+            return tile
+
+        tab_s = keep.tile([P, T], U8, name="tab_s")
+        nc.gpsimd.memset(tab_s[:].bitcast(I32), 0)
+        for quad in range(4):
+            nc.gpsimd.dma_start(
+                tab_s[32 * quad : 32 * quad + 8, :].bitcast(I32), tab_scales[:, 4 * quad : 4 * quad + 4, :].bitcast(I32)
+            )
+        idx = load_list(offs, "idx")
+        tab_w = [load_table_words(0)]
+        raw = [load_weight(w1[PASS * a : PASS * (a + 1), 0:PASS]) for a in range(PASSES)]
+        tab_w.append(load_table_words(1))
+        idx2 = load_list(offs2, "idx2")
+        base_t = {0: load_base(0)}
+        wgs_first = load_wgs(0, 1, "wgs_first")
+        page_t = {0: load_page(0)}
+
+        v_w = [keep.tile([P, S], U32, name="v_w%d" % a, align_bytes=64) for a in range(PASSES)]
+        v_s = keep.tile([P, S], U8, name="v_s", align_bytes=64)
+        nc.vector.tensor_copy(v_w[0][:], tab_w[0][:].bitcast(U32).indirect(idx[:]))
+        nc.vector.tensor_copy(v_s[:], tab_s[:].indirect(idx[:]))
+        w1_q = {(0, a): quantize_weight(raw[a], "w1_0%d" % a, True) for a in range(PASSES)}
+        for u in range(2):
+            nc.vector.tensor_copy(
+                v_w[1][:, BANK * u : BANK * (u + 1)], tab_w[1][:].bitcast(U32).indirect(idx[:, 32 * u : 32 * (u + 1)])
+            )
+
+        def product_with_v(acc, weights, col0, u):
+            for a in range(PASSES):
+                codes, scales = weights[a]
+                nc.tensor.matmul_mx(
+                    out=acc[:],
+                    lhsT=codes[:, col0 : col0 + P].bitcast(FP8X4),
+                    lhsT_scale=scales[:, col0 : col0 + P],
+                    rhs=v_w[a][:, BANK * u : BANK * (u + 1)].bitcast(FP8X4),
+                    rhs_scale=v_s[4 * a : P, BANK * u : BANK * (u + 1)],
+                    start=(a == 0),
+                    stop=(a == PASSES - 1),
+                )
+
+        idx3 = load_list(offs3, "idx3")
+        wgt_t = keep.tile([P, S], F32, name="wgt_t")
+        nc.sync.dma_start(wgt_t[:], wgt)
+        x_f = [keep.tile([P, PACK, S], F32, name="x_f%d" % g) for g in range(PASSES)]
+
+        def make_h(s):
+            g, t = divmod(s, PACK)
+            if s == PACK:
+                h = keep.tile([P, S], F32, name="h_hold", tag="hold", align_bytes=64)
+            else:
+                h = keep.tile([P, S], F32, name="h", tag="h", bufs=2)
+            for u in range(2):
+                acc = bank_tile(2 * (s % 2) + u, [P, BANK], "acc_h")
+                product_with_v(acc, [w1_q[(g, a)] for a in range(PASSES)], P * t, u)
+                cols = slice(BANK * u, BANK * (u + 1))
+                nc.vector.tensor_tensor(h[:, cols], acc[:], base_t[s][:, cols], ALU.max)
+            return h
+
+        def scatter(s, h, wgs_slice):
+            nc.vector.tensor_tensor(page_t[s][:].indirect(idx2[:]), h[:], wgs_slice, ALU.mult)
+
+        def gather(s, c0, c1):
+            g, t = divmod(s, PACK)
+            nc.vector.tensor_tensor(
+                x_f[g][:, t, c0:c1], page_t[s][:].indirect(idx3[:, c0 // 16 : c1 // 16]), wgt_t[:, c0:c1], ALU.mult
+            )
+
+        def round_x(g, c0, c1):
+            grouped = bf_tile(PACK * (c1 - c0))
+            nc.scalar.copy(
+                out=grouped[:].rearrange("p (c i t) -> p c t i", i=4, t=PACK),
+                in_=x_f[g][:, :, c0:c1].rearrange("p t (c i) -> p c t i", i=4),
+            )
+            return grouped
+
+        scatter(0, make_h(0), wgs_first[:, 0, :])
+        base_t[1] = load_base(1)
+        wgs_rest = load_wgs(1, PACK, "wgs_rest")
+        page_t[1] = load_page(1)
+        wgs_t = [wgs_first[:, 0, :]] + [wgs_rest[:, t, :] for t in range(PACK - 1)]
+        gather(0, 0, S)
+        scatter(1, make_h(1), wgs_t[1])
+        base_t[2] = load_base(2)
+        page_t[2] = load_page(2)
+        gather(1, 0, S)
+        for a in range(PASSES):
+            w1_q[(1, a)] = quantize_weight(load_weight(w1[PASS * a : PASS * (a + 1), PASS : 2 * PASS]), "w1_1%d" % a, True)
+        w2_q = [quantize_weight(load_weight(w2[PASS * a : PASS * (a + 1), :]), "w2_%d" % a, False) for a in range(PASSES)]
+        bias = keep.tile([P, N // P], F32, name="bias")
+        with nc.allow_non_contiguous_dma(reason="one bias value a partition"):
+            nc.sync.dma_start(bias[:], b.rearrange("(c p) -> p c", p=P))
+        scatter(2, make_h(2), wgs_t[2])
+        gather(2, 0, S)
+
+        res = keep.tile([P, N // P, S], F32, name="res")
+        for c in range(N // P):
+            for u in range(2):
+                acc = bank_tile(4 + 2 * (c % 2) + u, [P, BANK], "acc_d")
+                product_with_v(acc, w2_q, P * c, u)
+                nc.scalar.activation(res[:, c, BANK * u : BANK * (u + 1)], acc[:], ACT.Identity, bias=bias[:, c : c + 1])
+
+        base_t[3] = load_base(3)
+        page_t[3] = load_page(3)
+        scatter(3, make_h(3), wgs_t[3])
+        gather(3, 0, S)
+        x0_grouped = [round_x(0, BANK * u, BANK * (u + 1)) for u in range(2)]
+
+        base_t[4] = load_base(4)
+        page_t[4] = load_page(4)
+        w4_w = keep.tile([P, PASSES, 2 * N], U8, name="w4_w", align_bytes=64)
+        nc.sync.dma_start(w4_w[:].bitcast(I32), w4_words.rearrange("a p n -> p a n").bitcast(I32))
+        w4_s = keep.tile([P, PASSES, N], U8, name="w4_s", align_bytes=64)
+        nc.gpsimd.memset(w4_s[:].bitcast(I32), 0)
+        for quad in range(4):
+            nc.sync.dma_start(
+                w4_s[32 * quad : 32 * quad + 4, :, :].bitcast(I32),
+                w4_scales[:, 4 * quad : 4 * quad + 4, :].rearrange("a r n -> r a n").bitcast(I32),
+            )
+        scatter(4, make_h(4), wgs_t[0])
+        x_c = [keep.tile([P, S], U32, name="x_c0", tag="hold", align_bytes=64)]
+        x_c.append(keep.tile([P, S], U32, name="x_c1", align_bytes=64))
+        x_s = [keep.tile([P, S], U8, name="x_s%d" % g, align_bytes=64) for g in range(PASSES)]
+        for u in range(2):
+            cols = slice(BANK * u, BANK * (u + 1))
+            quantize(x0_grouped[u], x_c[0][:, cols], x_s[0][:, cols])
+        gather(4, 0, S)
+        for s in range(5, SLICES):
+            base_t[s] = load_base(s)
+            page_t[s] = load_page(s)
+            scatter(s, make_h(s), wgs_t[s % PACK])
+            if s < SLICES - 1:
+                gather(s, 0, S)
+
+        def y_pass(acc, pair, g, cols, start, stop):
+            for e in range(2):
+                c = 2 * pair + e
+                nc.tensor.matmul_mx(
+                    out=acc[:, e, :],
+                    lhsT=w4_w[:, g, 2 * P * c : 2 * P * (c + 1)].bitcast(FP4X4),
+                    lhsT_scale=w4_s[:, g, P * c : P * (c + 1)],
+                    rhs=x_c[g][:, cols].bitcast(FP8X4),
+                    rhs_scale=x_s[g][:, cols],
+                    start=start and e == 0,
+                    stop=stop and e == 1,
+                )
+
+        chunks = [slice(c0, c0 + CHUNK) for c0 in range(0, S, CHUNK)]
+        y_acc = {}
+        for i, cols in enumerate(chunks):
+            for pair in range(2):
+                y_acc[(i, pair)] = bank_tile((4 + 2 * i + pair) % 8, [P, 2, CHUNK], "acc_y")
+                y_pass(y_acc[(i, pair)], pair, 0, cols, True, False)
+        for cols in chunks:
+            gather(SLICES - 1, cols.start, cols.stop)
+        out_rows = out.rearrange("(c p) m -> p c m", p=P)
+        for i, cols in enumerate(chunks):
+            quantize(round_x(1, cols.start, cols.stop), x_c[1][:, cols], x_s[1][:, cols])
+            for pair in range(2):
+                y_pass(y_acc[(i, pair)], pair, 1, cols, False, True)
+                for e in range(2):
+                    c = 2 * pair + e
+                    nc.vector.scalar_tensor_tensor(
+                        res[:, c, cols], y_acc[(i, pair)][:, e, :], bias[:, c : c + 1], res[:, c, cols], ALU.add, ALU.max
+                    )
+            nc.sync.dma_start(out_rows[:, :, cols], res[:, :, cols])

@@ -1,6 +1,7 @@
 from contextlib import ExitStack
 
 import concourse.mybir as mybir
+from concourse.masks import make_identity
 
 K, H, N, T, S, T2 = 1024, 1024, 512, 2048, 1024, 2048
 FLOPS = 2 * K * H * S + 2 * H * N * S + 2 * K * N * S
@@ -23,6 +24,7 @@ PASSES = 2
 BANK = 512
 SLICES = PASSES * PACK
 CHUNK = 256
+ON_VECTOR = (0, 1)
 
 
 def tile_list_rotor_fault_scores_kernel(
@@ -58,151 +60,199 @@ def tile_list_rotor_fault_scores_kernel(
             nc.vector.quantize_mx(out=codes.bitcast(FP8X4), scales=scales, in_=grouped[:])
 
         def quantize_weight(raw, name, dealt):
-            grouped = bf_tile(PACK * PASS)
+            t0, t1 = dealt or (0, PACK)
+            grouped = bf_tile(PACK * P * (t1 - t0))
             if dealt:
                 nc.scalar.copy(
-                    out=grouped[:].rearrange("p (t m j) -> p m j t", t=PACK, j=PACK),
-                    in_=raw[:].rearrange("p j (m t) -> p m j t", t=PACK),
+                    out=grouped[:].rearrange("p (t m j) -> p m j t", t=t1 - t0, j=PACK),
+                    in_=raw[:].rearrange("p j (m t) -> p m j t", t=PACK)[:, :, :, t0:t1],
                 )
             else:
                 nc.scalar.copy(
                     out=grouped[:].rearrange("p (c i j) -> p c j i", i=4, j=PACK),
                     in_=raw[:].rearrange("p j (c i) -> p c j i", i=4),
                 )
-            codes = keep.tile([P, PASS], U32, name=name + "_c", align_bytes=64)
-            scales = keep.tile([P, PASS], U8, name=name + "_s", align_bytes=64)
+            codes = keep.tile([P, P * (t1 - t0)], U32, name=name + "_c", align_bytes=64)
+            scales = keep.tile([P, P * (t1 - t0)], U8, name=name + "_s", align_bytes=64)
             quantize(grouped, codes[:], scales[:])
-            return codes, scales
+            return [(codes[:, P * i : P * (i + 1)], scales[:, P * i : P * (i + 1)]) for i in range(t1 - t0)]
 
         def slice_rows(src, s):
             rows = src[PASS * (s // PACK) : PASS * (s // PACK + 1), :]
             return rows.rearrange("(p t) j -> p t j", t=PACK)[:, s % PACK, :]
 
-        def load_base(s):
-            tile = keep.tile([P, S], F32, name="base", tag="base", bufs=4)
-            nc.sync.dma_start(tile[:], slice_rows(base, s))
-            return tile
-
         def load_page(s):
-            tile = keep.tile([P, T2], F32, name="page", tag="page", bufs=6)
+            tile = keep.tile([P, T2], F32, name="page", tag="page", bufs=5)
             nc.sync.dma_start(tile[:], slice_rows(page0, s))
             return tile
 
         wgs_rows = wgs.rearrange("(q t) j -> q t j", t=PACK)
 
-        def load_wgs(t0, t1, name):
-            tile = keep.tile([P, t1 - t0, S], F32, name=name)
+        def load_wgs(t):
+            tile = keep.tile([P, S], F32, name="wgs%d" % t)
             for quad in (0, 2, 1, 3):
-                nc.sync.dma_start(tile[32 * quad : 32 * quad + 32, :, :], wgs_rows[:, t0:t1, :])
+                nc.sync.dma_start(tile[32 * quad : 32 * quad + 32, :], wgs_rows[:, t, :])
             return tile
+
+        x_f = [keep.tile([P, PACK, S], F32, name="x_f%d" % g) for g in range(PASSES)]
+
+        def x_plane(s):
+            return x_f[s // PACK][:, s % PACK, :]
+
+        def load_base(s):
+            if s in ON_VECTOR:
+                rows = keep.tile([P, S], F32, name="base%d" % s)[:]
+            else:
+                rows = x_plane(s - 2)
+            nc.sync.dma_start(rows, slice_rows(base, s))
+            return rows
 
         tab_s = keep.tile([P, T], U8, name="tab_s")
         nc.gpsimd.memset(tab_s[:].bitcast(I32), 0)
         for quad in range(4):
-            nc.gpsimd.dma_start(
+            nc.scalar.dma_start(
                 tab_s[32 * quad : 32 * quad + 8, :].bitcast(I32), tab_scales[:, 4 * quad : 4 * quad + 4, :].bitcast(I32)
             )
         idx = load_list(offs, "idx")
-        tab_w = [load_table_words(0)]
-        raw = [load_weight(w1[PASS * a : PASS * (a + 1), 0:PASS]) for a in range(PASSES)]
-        tab_w.append(load_table_words(1))
         idx2 = load_list(offs2, "idx2")
+        idx3 = load_list(offs3, "idx3")
+        tab_w = [load_table_words(0)]
+        raw = [load_weight(w1[0:PASS, 0:PASS])]
+        tab_w.append(load_table_words(1))
+        raw.append(load_weight(w1[PASS : 2 * PASS, 0:PASS]))
         base_t = {0: load_base(0)}
-        wgs_first = load_wgs(0, 1, "wgs_first")
         page_t = {0: load_page(0)}
+        wgs_t = [load_wgs(0)]
+        ident = keep.tile([P, P], F32, name="ident")
+        make_identity(nc, ident[:])
 
         v_w = [keep.tile([P, S], U32, name="v_w%d" % a, align_bytes=64) for a in range(PASSES)]
         v_s = keep.tile([P, S], U8, name="v_s", align_bytes=64)
         nc.vector.tensor_copy(v_w[0][:], tab_w[0][:].bitcast(U32).indirect(idx[:]))
         nc.vector.tensor_copy(v_s[:], tab_s[:].indirect(idx[:]))
-        w1_q = {(0, a): quantize_weight(raw[a], "w1_0%d" % a, True) for a in range(PASSES)}
-        for u in range(2):
-            nc.vector.tensor_copy(
-                v_w[1][:, BANK * u : BANK * (u + 1)], tab_w[1][:].bitcast(U32).indirect(idx[:, 32 * u : 32 * (u + 1)])
-            )
+        w1_q = {(0, 0): quantize_weight(raw[0], "w1_00a", (0, 2))}
+        nc.vector.tensor_copy(v_w[1][:], tab_w[1][:].bitcast(U32).indirect(idx[:]))
+        w1_q[(0, 1)] = quantize_weight(raw[1], "w1_01a", (0, 2))
 
-        def product_with_v(acc, weights, col0, u):
+        def product_with_v(acc, weights, u):
             for a in range(PASSES):
                 codes, scales = weights[a]
                 nc.tensor.matmul_mx(
                     out=acc[:],
-                    lhsT=codes[:, col0 : col0 + P].bitcast(FP8X4),
-                    lhsT_scale=scales[:, col0 : col0 + P],
+                    lhsT=codes.bitcast(FP8X4),
+                    lhsT_scale=scales,
                     rhs=v_w[a][:, BANK * u : BANK * (u + 1)].bitcast(FP8X4),
                     rhs_scale=v_s[4 * a : P, BANK * u : BANK * (u + 1)],
                     start=(a == 0),
                     stop=(a == PASSES - 1),
                 )
 
-        idx3 = load_list(offs3, "idx3")
-        wgt_t = keep.tile([P, S], F32, name="wgt_t")
-        nc.sync.dma_start(wgt_t[:], wgt)
-        x_f = [keep.tile([P, PACK, S], F32, name="x_f%d" % g) for g in range(PASSES)]
+        def turn_blocks(acc, src, start, stop):
+            for i in range(BANK // P):
+                nc.tensor.matmul(
+                    acc[:, P * i : P * (i + 1)],
+                    lhsT=src[:, P * i : P * (i + 1)],
+                    rhs=ident[:],
+                    is_transpose=True,
+                    start=start and i == 0,
+                    stop=stop and i == BANK // P - 1,
+                )
+
+        def half_tile(name):
+            return keep.tile([P, BANK], F32, name=name, tag=name, bufs=2)
 
         def make_h(s):
             g, t = divmod(s, PACK)
-            if s == PACK:
-                h = keep.tile([P, S], F32, name="h_hold", tag="hold", align_bytes=64)
-            else:
-                h = keep.tile([P, S], F32, name="h", tag="h", bufs=2)
+            h = keep.tile([P, S], F32, name="h", tag="h", bufs=3)
             for u in range(2):
-                acc = bank_tile(2 * (s % 2) + u, [P, BANK], "acc_h")
-                product_with_v(acc, [w1_q[(g, a)] for a in range(PASSES)], P * t, u)
                 cols = slice(BANK * u, BANK * (u + 1))
-                nc.vector.tensor_tensor(h[:, cols], acc[:], base_t[s][:, cols], ALU.max)
+                acc = bank_tile(4 + 2 * s + u if s < 2 else u, [P, BANK], "acc_a")
+                product_with_v(acc, [w1_q[(g, a)][t] for a in range(PASSES)], u)
+                if s in ON_VECTOR:
+                    nc.vector.tensor_tensor(h[:, cols], acc[:], base_t[s][:, cols], ALU.max)
+                    continue
+                neg_a = half_tile("neg_a")
+                nc.scalar.activation(neg_a[:], acc[:], ACT.Copy, scale=-1.0)
+                turned = bank_tile(2 + u, [P, BANK], "acc_t")
+                turn_blocks(turned, neg_a, True, True)
+                a_t = half_tile("a_t")
+                nc.scalar.activation(a_t[:], turned[:], ACT.Copy, scale=-1.0)
+                diff = bank_tile(4 + u, [P, BANK], "acc_diff")
+                turn_blocks(diff, neg_a, True, False)
+                turn_blocks(diff, base_t[s][:, cols], False, True)
+                if s == 6:
+                    lift_t = keep.tile([P, BANK], F32, name="lift_hold", tag="hold%d" % u, align_bytes=64)[:]
+                elif s == 7:
+                    lift_t = x_plane(6)[:, cols]
+                else:
+                    lift_t = half_tile("lift_t")[:]
+                nc.scalar.activation(lift_t, diff[:], ACT.Relu)
+                back = bank_tile(6 + u, [P, BANK], "acc_h")
+                turn_blocks(back, a_t, True, False)
+                turn_blocks(back, lift_t, False, True)
+                nc.scalar.copy(h[:, cols], back[:])
             return h
 
-        def scatter(s, h, wgs_slice):
-            nc.vector.tensor_tensor(page_t[s][:].indirect(idx2[:]), h[:], wgs_slice, ALU.mult)
+        def scatter(s, h):
+            nc.vector.tensor_tensor(page_t[s][:].indirect(idx2[:]), h[:], wgs_t[s % PACK][:], ALU.mult)
 
         def gather(s, c0, c1):
-            g, t = divmod(s, PACK)
             nc.vector.tensor_tensor(
-                x_f[g][:, t, c0:c1], page_t[s][:].indirect(idx3[:, c0 // 16 : c1 // 16]), wgt_t[:, c0:c1], ALU.mult
+                x_plane(s)[:, c0:c1], page_t[s][:].indirect(idx3[:, c0 // 16 : c1 // 16]), wgt_t[:, c0:c1], ALU.mult
             )
 
-        def round_x(g, c0, c1):
-            grouped = bf_tile(PACK * (c1 - c0))
+        def round_x(grouped, g, c0, c1):
             nc.scalar.copy(
                 out=grouped[:].rearrange("p (c i t) -> p c t i", i=4, t=PACK),
                 in_=x_f[g][:, :, c0:c1].rearrange("p t (c i) -> p c t i", i=4),
             )
             return grouped
 
-        scatter(0, make_h(0), wgs_first[:, 0, :])
+        scatter(0, make_h(0))
         base_t[1] = load_base(1)
-        wgs_rest = load_wgs(1, PACK, "wgs_rest")
         page_t[1] = load_page(1)
-        wgs_t = [wgs_first[:, 0, :]] + [wgs_rest[:, t, :] for t in range(PACK - 1)]
-        gather(0, 0, S)
-        scatter(1, make_h(1), wgs_t[1])
-        base_t[2] = load_base(2)
-        page_t[2] = load_page(2)
-        gather(1, 0, S)
+        wgs_t.append(load_wgs(1))
+        h = make_h(1)
         for a in range(PASSES):
-            w1_q[(1, a)] = quantize_weight(load_weight(w1[PASS * a : PASS * (a + 1), PASS : 2 * PASS]), "w1_1%d" % a, True)
-        w2_q = [quantize_weight(load_weight(w2[PASS * a : PASS * (a + 1), :]), "w2_%d" % a, False) for a in range(PASSES)]
-        bias = keep.tile([P, N // P], F32, name="bias")
-        with nc.allow_non_contiguous_dma(reason="one bias value a partition"):
-            nc.sync.dma_start(bias[:], b.rearrange("(c p) -> p c", p=P))
-        scatter(2, make_h(2), wgs_t[2])
-        gather(2, 0, S)
+            w1_q[(0, a)].extend(quantize_weight(raw[a], "w1_0%db" % a, (2, PACK)))
+        scatter(1, h)
+        wgt_t = keep.tile([P, S], F32, name="wgt_t")
+        nc.sync.dma_start(wgt_t[:], wgt)
 
-        res = keep.tile([P, N // P, S], F32, name="res")
-        for c in range(N // P):
-            for u in range(2):
-                acc = bank_tile(4 + 2 * (c % 2) + u, [P, BANK], "acc_d")
-                product_with_v(acc, w2_q, P * c, u)
-                nc.scalar.activation(res[:, c, BANK * u : BANK * (u + 1)], acc[:], ACT.Identity, bias=bias[:, c : c + 1])
+        base_t[2] = load_base(2)
+        wgs_t.append(load_wgs(2))
+        h = make_h(2)
+        gather(0, 0, S)
+        for a in range(PASSES):
+            w1_q[(1, a)] = quantize_weight(load_weight(w1[PASS * a : PASS * (a + 1), PASS : 2 * PASS]), "w1_1%d" % a, (0, PACK))
+        page_t[2] = load_page(2)
+        scatter(2, h)
 
         base_t[3] = load_base(3)
+        wgs_t.append(load_wgs(3))
         page_t[3] = load_page(3)
-        scatter(3, make_h(3), wgs_t[3])
-        gather(3, 0, S)
-        x0_grouped = [round_x(0, BANK * u, BANK * (u + 1)) for u in range(2)]
+        h = make_h(3)
+        gather(1, 0, S)
+        scatter(3, h)
 
         base_t[4] = load_base(4)
         page_t[4] = load_page(4)
+        h = make_h(4)
+        gather(2, 0, S)
+        scatter(4, h)
+
+        base_t[5] = load_base(5)
+        h = make_h(5)
+        gather(3, 0, S)
+        w2_q = [quantize_weight(load_weight(w2[PASS * a : PASS * (a + 1), :]), "w2_%d" % a, None) for a in range(PASSES)]
+        page_t[5] = load_page(5)
+        scatter(5, h)
+        bias = keep.tile([P, N // P], F32, name="bias")
+        with nc.allow_non_contiguous_dma(reason="one bias value a partition"):
+            nc.sync.dma_start(bias[:], b.rearrange("(c p) -> p c", p=P))
+
+        base_t[6] = load_base(6)
+        page_t[6] = load_page(6)
         w4_w = keep.tile([P, PASSES, 2 * N], U8, name="w4_w", align_bytes=64)
         nc.sync.dma_start(w4_w[:].bitcast(I32), w4_words.rearrange("a p n -> p a n").bitcast(I32))
         w4_s = keep.tile([P, PASSES, N], U8, name="w4_s", align_bytes=64)
@@ -212,20 +262,30 @@ def tile_list_rotor_fault_scores_kernel(
                 w4_s[32 * quad : 32 * quad + 4, :, :].bitcast(I32),
                 w4_scales[:, 4 * quad : 4 * quad + 4, :].rearrange("a r n -> r a n").bitcast(I32),
             )
-        scatter(4, make_h(4), wgs_t[0])
-        x_c = [keep.tile([P, S], U32, name="x_c0", tag="hold", align_bytes=64)]
-        x_c.append(keep.tile([P, S], U32, name="x_c1", align_bytes=64))
+        h = make_h(6)
+        gather(4, 0, S)
+        scatter(6, h)
+
+        x_c = [keep.tile([P, S], U32, name="x_c%d" % g, align_bytes=64) for g in range(PASSES)]
         x_s = [keep.tile([P, S], U8, name="x_s%d" % g, align_bytes=64) for g in range(PASSES)]
         for u in range(2):
             cols = slice(BANK * u, BANK * (u + 1))
-            quantize(x0_grouped[u], x_c[0][:, cols], x_s[0][:, cols])
-        gather(4, 0, S)
-        for s in range(5, SLICES):
-            base_t[s] = load_base(s)
-            page_t[s] = load_page(s)
-            scatter(s, make_h(s), wgs_t[s % PACK])
-            if s < SLICES - 1:
-                gather(s, 0, S)
+            grouped = keep.tile([P, PACK * BANK], BF16, name="x0_bf", tag="hold%d" % u, align_bytes=64)
+            quantize(round_x(grouped, 0, cols.start, cols.stop), x_c[0][:, cols], x_s[0][:, cols])
+
+        base_t[7] = load_base(7)
+        page_t[7] = load_page(7)
+        h = make_h(7)
+        gather(5, 0, S)
+        gather(6, 0, S)
+        scatter(7, h)
+
+        res = keep.tile([P, N // P, S], F32, name="res")
+        for c in range(N // P):
+            for u in range(2):
+                acc = bank_tile(u, [P, BANK], "acc_d")
+                product_with_v(acc, [w2_q[a][c] for a in range(PASSES)], u)
+                nc.scalar.activation(res[:, c, BANK * u : BANK * (u + 1)], acc[:], ACT.Identity, bias=bias[:, c : c + 1])
 
         def y_pass(acc, pair, g, cols, start, stop):
             for e in range(2):
@@ -244,13 +304,13 @@ def tile_list_rotor_fault_scores_kernel(
         y_acc = {}
         for i, cols in enumerate(chunks):
             for pair in range(2):
-                y_acc[(i, pair)] = bank_tile((4 + 2 * i + pair) % 8, [P, 2, CHUNK], "acc_y")
+                y_acc[(i, pair)] = bank_tile((2 + 2 * i + pair) % 8, [P, 2, CHUNK], "acc_y")
                 y_pass(y_acc[(i, pair)], pair, 0, cols, True, False)
         for cols in chunks:
             gather(SLICES - 1, cols.start, cols.stop)
         out_rows = out.rearrange("(c p) m -> p c m", p=P)
         for i, cols in enumerate(chunks):
-            quantize(round_x(1, cols.start, cols.stop), x_c[1][:, cols], x_s[1][:, cols])
+            quantize(round_x(bf_tile(PACK * CHUNK), 1, cols.start, cols.stop), x_c[1][:, cols], x_s[1][:, cols])
             for pair in range(2):
                 y_pass(y_acc[(i, pair)], pair, 1, cols, False, True)
                 for e in range(2):
@@ -258,4 +318,4 @@ def tile_list_rotor_fault_scores_kernel(
                     nc.vector.scalar_tensor_tensor(
                         res[:, c, cols], y_acc[(i, pair)][:, e, :], bias[:, c : c + 1], res[:, c, cols], ALU.add, ALU.max
                     )
-            nc.sync.dma_start(out_rows[:, :, cols], res[:, :, cols])
+                nc.sync.dma_start(out_rows[:, 2 * pair : 2 * pair + 2, cols], res[:, 2 * pair : 2 * pair + 2, cols])

@@ -24,7 +24,7 @@ PASSES = 2
 BANK = 512
 SLICES = PASSES * PACK
 CHUNK = 256
-ON_VECTOR = (0, 1)
+ON_VECTOR = (0, 1, 4)
 
 
 def tile_list_rotor_fault_scores_kernel(
@@ -54,7 +54,7 @@ def tile_list_rotor_fault_scores_kernel(
             return raw
 
         def bf_tile(width):
-            return keep.tile([P, width], BF16, name="bf", tag="bf", bufs=3, align_bytes=64)
+            return keep.tile([P, width], BF16, name="bf", tag="bf", bufs=4, align_bytes=64)
 
         def quantize(grouped, codes, scales):
             nc.vector.quantize_mx(out=codes.bitcast(FP8X4), scales=scales, in_=grouped[:])
@@ -101,7 +101,7 @@ def tile_list_rotor_fault_scores_kernel(
 
         def load_base(s):
             if s in ON_VECTOR:
-                rows = keep.tile([P, S], F32, name="base%d" % s)[:]
+                rows = keep.tile([P, S], F32, name="base", tag="base", bufs=2)[:]
             else:
                 rows = x_plane(s - 2)
             nc.sync.dma_start(rows, slice_rows(base, s))
@@ -164,26 +164,34 @@ def tile_list_rotor_fault_scores_kernel(
         def make_h(s):
             g, t = divmod(s, PACK)
             h = keep.tile([P, S], F32, name="h", tag="h", bufs=3)
+            if s == 5:
+                a_t_both = keep.tile([P, S], F32, name="a_t_both", tag="raw", bufs=2)
+                neg_a_both = keep.tile([P, S], F32, name="neg_a_both", tag="raw", bufs=2)
             for u in range(2):
                 cols = slice(BANK * u, BANK * (u + 1))
-                acc = bank_tile(4 + 2 * s + u if s < 2 else u, [P, BANK], "acc_a")
+                acc = bank_tile({0: 4, 1: 6, 4: 2}.get(s, 0) + u, [P, BANK], "acc_a")
                 product_with_v(acc, [w1_q[(g, a)][t] for a in range(PASSES)], u)
                 if s in ON_VECTOR:
                     nc.vector.tensor_tensor(h[:, cols], acc[:], base_t[s][:, cols], ALU.max)
                     continue
-                neg_a = half_tile("neg_a")
-                nc.scalar.activation(neg_a[:], acc[:], ACT.Copy, scale=-1.0)
+                if (s, u) == (SLICES - 1, 1):
+                    neg_a = keep.tile([P, BANK], F32, name="neg_a_last", tag="hold_codes", align_bytes=64)[:]
+                elif s == 5:
+                    neg_a = neg_a_both[:, cols]
+                else:
+                    neg_a = half_tile("neg_a")[:]
+                nc.scalar.activation(neg_a, acc[:], ACT.Copy, scale=-1.0)
                 turned = bank_tile(2 + u, [P, BANK], "acc_t")
                 turn_blocks(turned, neg_a, True, True)
-                a_t = half_tile("a_t")
-                nc.scalar.activation(a_t[:], turned[:], ACT.Copy, scale=-1.0)
+                a_t = a_t_both[:, cols] if s == 5 else half_tile("a_t")[:]
+                nc.scalar.activation(a_t, turned[:], ACT.Copy, scale=-1.0)
                 diff = bank_tile(4 + u, [P, BANK], "acc_diff")
                 turn_blocks(diff, neg_a, True, False)
                 turn_blocks(diff, base_t[s][:, cols], False, True)
                 if s == 6:
                     lift_t = keep.tile([P, BANK], F32, name="lift_hold", tag="hold%d" % u, align_bytes=64)[:]
-                elif s == 7:
-                    lift_t = x_plane(6)[:, cols]
+                elif s in (3, 7):
+                    lift_t = x_plane(s - 1)[:, cols]
                 else:
                     lift_t = half_tile("lift_t")[:]
                 nc.scalar.activation(lift_t, diff[:], ACT.Relu)
@@ -230,26 +238,34 @@ def tile_list_rotor_fault_scores_kernel(
 
         base_t[3] = load_base(3)
         wgs_t.append(load_wgs(3))
+        base_t[4] = load_base(4)
+        w2_raw = [load_weight(w2[PASS * a : PASS * (a + 1), :]) for a in range(PASSES)]
         page_t[3] = load_page(3)
         h = make_h(3)
         gather(1, 0, S)
+        gather(2, 0, S)
+        h_next = make_h(4)
+        w2_q = [quantize_weight(w2_raw[a], "w2_%d" % a, None) for a in range(PASSES)]
         scatter(3, h)
 
-        base_t[4] = load_base(4)
         page_t[4] = load_page(4)
-        h = make_h(4)
-        gather(2, 0, S)
-        scatter(4, h)
-
         base_t[5] = load_base(5)
-        h = make_h(5)
-        gather(3, 0, S)
-        w2_q = [quantize_weight(load_weight(w2[PASS * a : PASS * (a + 1), :]), "w2_%d" % a, None) for a in range(PASSES)]
-        page_t[5] = load_page(5)
-        scatter(5, h)
+        scatter(4, h_next)
         bias = keep.tile([P, N // P], F32, name="bias")
         with nc.allow_non_contiguous_dma(reason="one bias value a partition"):
             nc.sync.dma_start(bias[:], b.rearrange("(c p) -> p c", p=P))
+
+        h = make_h(5)
+        gather(3, 0, S)
+        res = keep.tile([P, N // P, S], F32, name="res")
+        for c in range(N // P):
+            for u in range(2):
+                acc = bank_tile(6 + u, [P, BANK], "acc_d")
+                product_with_v(acc, [w2_q[a][c] for a in range(PASSES)], u)
+                nc.scalar.activation(res[:, c, BANK * u : BANK * (u + 1)], acc[:], ACT.Identity, bias=bias[:, c : c + 1])
+
+        page_t[5] = load_page(5)
+        scatter(5, h)
 
         base_t[6] = load_base(6)
         page_t[6] = load_page(6)
@@ -266,26 +282,23 @@ def tile_list_rotor_fault_scores_kernel(
         gather(4, 0, S)
         scatter(6, h)
 
-        x_c = [keep.tile([P, S], U32, name="x_c%d" % g, align_bytes=64) for g in range(PASSES)]
-        x_s = [keep.tile([P, S], U8, name="x_s%d" % g, align_bytes=64) for g in range(PASSES)]
+        x0_grouped = []
         for u in range(2):
-            cols = slice(BANK * u, BANK * (u + 1))
             grouped = keep.tile([P, PACK * BANK], BF16, name="x0_bf", tag="hold%d" % u, align_bytes=64)
-            quantize(round_x(grouped, 0, cols.start, cols.stop), x_c[0][:, cols], x_s[0][:, cols])
+            x0_grouped.append(round_x(grouped, 0, BANK * u, BANK * (u + 1)))
 
         base_t[7] = load_base(7)
         page_t[7] = load_page(7)
         h = make_h(7)
         gather(5, 0, S)
+        x_c = [keep.tile([P, S], U32, name="x_c0", tag="hold_codes", align_bytes=64)]
+        x_c.append(keep.tile([P, S], U32, name="x_c1", align_bytes=64))
+        x_s = [keep.tile([P, S], U8, name="x_s%d" % g, align_bytes=64) for g in range(PASSES)]
+        for u in range(2):
+            cols = slice(BANK * u, BANK * (u + 1))
+            quantize(x0_grouped[u], x_c[0][:, cols], x_s[0][:, cols])
         gather(6, 0, S)
         scatter(7, h)
-
-        res = keep.tile([P, N // P, S], F32, name="res")
-        for c in range(N // P):
-            for u in range(2):
-                acc = bank_tile(u, [P, BANK], "acc_d")
-                product_with_v(acc, [w2_q[a][c] for a in range(PASSES)], u)
-                nc.scalar.activation(res[:, c, BANK * u : BANK * (u + 1)], acc[:], ACT.Identity, bias=bias[:, c : c + 1])
 
         def y_pass(acc, pair, g, cols, start, stop):
             for e in range(2):
@@ -304,7 +317,7 @@ def tile_list_rotor_fault_scores_kernel(
         y_acc = {}
         for i, cols in enumerate(chunks):
             for pair in range(2):
-                y_acc[(i, pair)] = bank_tile((2 + 2 * i + pair) % 8, [P, 2, CHUNK], "acc_y")
+                y_acc[(i, pair)] = bank_tile(2 * i + pair, [P, 2, CHUNK], "acc_y")
                 y_pass(y_acc[(i, pair)], pair, 0, cols, True, False)
         for cols in chunks:
             gather(SLICES - 1, cols.start, cols.stop)

@@ -64,13 +64,13 @@ def tile_list_rotor_fault_scores_kernel(
             grouped = bf_tile(PACK * P * (t1 - t0))
             if dealt:
                 nc.scalar.copy(
-                    out=grouped[:].rearrange("p (t m j) -> p m j t", t=t1 - t0, j=PACK),
-                    in_=raw[:].rearrange("p j (m t) -> p m j t", t=PACK)[:, :, :, t0:t1],
+                    out=grouped[:].rearrange("p (t m j) -> p m t j", t=t1 - t0, j=PACK),
+                    in_=raw[:].rearrange("p j (m t) -> p m t j", t=PACK)[:, :, t0:t1, :],
                 )
             else:
                 nc.scalar.copy(
-                    out=grouped[:].rearrange("p (c i j) -> p c j i", i=4, j=PACK),
-                    in_=raw[:].rearrange("p j (c i) -> p c j i", i=4),
+                    out=grouped[:].rearrange("p (c j) -> p c j", j=PACK),
+                    in_=raw[:].rearrange("p j c -> p c j"),
                 )
             codes = keep.tile([P, P * (t1 - t0)], U32, name=name + "_c", align_bytes=64)
             scales = keep.tile([P, P * (t1 - t0)], U8, name=name + "_s", align_bytes=64)
@@ -211,8 +211,8 @@ def tile_list_rotor_fault_scores_kernel(
 
         def round_x(grouped, g, c0, c1):
             nc.scalar.copy(
-                out=grouped[:].rearrange("p (c i t) -> p c t i", i=4, t=PACK),
-                in_=x_f[g][:, :, c0:c1].rearrange("p t (c i) -> p c t i", i=4),
+                out=grouped[:].rearrange("p (c t) -> p c t", t=PACK),
+                in_=x_f[g][:, :, c0:c1].rearrange("p t c -> p c t"),
             )
             return grouped
 
@@ -322,13 +322,25 @@ def tile_list_rotor_fault_scores_kernel(
         for cols in chunks:
             gather(SLICES - 1, cols.start, cols.stop)
         out_rows = out.rearrange("(c p) m -> p c m", p=P)
-        for i, cols in enumerate(chunks):
+
+        def finish_product(i):
+            cols = chunks[i]
             quantize(round_x(bf_tile(PACK * CHUNK), 1, cols.start, cols.stop), x_c[1][:, cols], x_s[1][:, cols])
             for pair in range(2):
                 y_pass(y_acc[(i, pair)], pair, 1, cols, False, True)
+
+        def finish_scores(i):
+            cols = chunks[i]
+            for pair in range(2):
                 for e in range(2):
                     c = 2 * pair + e
                     nc.vector.scalar_tensor_tensor(
                         res[:, c, cols], y_acc[(i, pair)][:, e, :], bias[:, c : c + 1], res[:, c, cols], ALU.add, ALU.max
                     )
                 nc.sync.dma_start(out_rows[:, 2 * pair : 2 * pair + 2, cols], res[:, 2 * pair : 2 * pair + 2, cols])
+
+        finish_product(0)
+        for i in range(len(chunks)):
+            if i + 1 < len(chunks):
+                finish_product(i + 1)
+            finish_scores(i)

@@ -88,11 +88,11 @@ def tile_list_rotor_fault_scores_kernel(
 
         wgs_rows = wgs.rearrange("(q t) j -> q t j", t=PACK)
 
-        def load_wgs(t):
-            tile = keep.tile([P, S], F32, name="wgs%d" % t)
+        wgs_t = [keep.tile([P, S], F32, name="wgs%d" % t) for t in range(PACK)]
+
+        def load_wgs(t, cols=slice(0, S)):
             for quad in (0, 2, 1, 3):
-                nc.sync.dma_start(tile[32 * quad : 32 * quad + 32, :], wgs_rows[:, t, :])
-            return tile
+                nc.sync.dma_start(wgs_t[t][32 * quad : 32 * quad + 32, cols], wgs_rows[:, t, cols])
 
         x_f = [keep.tile([P, PACK, S], F32, name="x_f%d" % g) for g in range(PASSES)]
 
@@ -120,9 +120,13 @@ def tile_list_rotor_fault_scores_kernel(
         raw = [load_weight(w1[0:PASS, 0:PASS])]
         tab_w.append(load_table_words(1))
         raw.append(load_weight(w1[PASS : 2 * PASS, 0:PASS]))
-        base_t = {0: load_base(0)}
+        halves = [slice(BANK * u, BANK * (u + 1)) for u in range(2)]
+        base_t = {0: keep.tile([P, S], F32, name="base", tag="base", bufs=2)[:]}
+        nc.sync.dma_start(base_t[0][:, halves[0]], slice_rows(base, 0)[:, halves[0]])
         page_t = {0: load_page(0)}
-        wgs_t = [load_wgs(0)]
+        load_wgs(0, halves[0])
+        nc.sync.dma_start(base_t[0][:, halves[1]], slice_rows(base, 0)[:, halves[1]])
+        load_wgs(0, halves[1])
         ident = keep.tile([P, P], F32, name="ident")
         make_identity(nc, ident[:])
 
@@ -169,7 +173,7 @@ def tile_list_rotor_fault_scores_kernel(
                 neg_a_both = keep.tile([P, S], F32, name="neg_a_both", tag="raw", bufs=2)
             for u in range(2):
                 cols = slice(BANK * u, BANK * (u + 1))
-                acc = bank_tile({0: 4, 1: 6, 4: 2}.get(s, 0) + u, [P, BANK], "acc_a")
+                acc = bank_tile({0: 4, 1: 4, 4: 2}.get(s, 0) + u, [P, BANK], "acc_a")
                 product_with_v(acc, [w1_q[(g, a)][t] for a in range(PASSES)], u)
                 if s in ON_VECTOR:
                     nc.vector.tensor_tensor(h[:, cols], acc[:], base_t[s][:, cols], ALU.max)
@@ -201,8 +205,9 @@ def tile_list_rotor_fault_scores_kernel(
                 nc.scalar.copy(h[:, cols], back[:])
             return h
 
-        def scatter(s, h):
-            nc.vector.tensor_tensor(page_t[s][:].indirect(idx2[:]), h[:], wgs_t[s % PACK][:], ALU.mult)
+        def scatter(s, h, cols=slice(0, S)):
+            places = idx2[:, cols.start // 16 : cols.stop // 16]
+            nc.vector.tensor_tensor(page_t[s][:].indirect(places), h[:, cols], wgs_t[s % PACK][:, cols], ALU.mult)
 
         def gather(s, c0, c1):
             nc.vector.tensor_tensor(
@@ -216,10 +221,12 @@ def tile_list_rotor_fault_scores_kernel(
             )
             return grouped
 
-        scatter(0, make_h(0))
+        h = make_h(0)
+        for cols in halves:
+            scatter(0, h, cols)
         base_t[1] = load_base(1)
         page_t[1] = load_page(1)
-        wgs_t.append(load_wgs(1))
+        load_wgs(1)
         h = make_h(1)
         for a in range(PASSES):
             w1_q[(0, a)].extend(quantize_weight(raw[a], "w1_0%db" % a, (2, PACK)))
@@ -228,7 +235,7 @@ def tile_list_rotor_fault_scores_kernel(
         nc.sync.dma_start(wgt_t[:], wgt)
 
         base_t[2] = load_base(2)
-        wgs_t.append(load_wgs(2))
+        load_wgs(2)
         h = make_h(2)
         gather(0, 0, S)
         for a in range(PASSES):
@@ -237,7 +244,7 @@ def tile_list_rotor_fault_scores_kernel(
         scatter(2, h)
 
         base_t[3] = load_base(3)
-        wgs_t.append(load_wgs(3))
+        load_wgs(3)
         base_t[4] = load_base(4)
         w2_raw = [load_weight(w2[PASS * a : PASS * (a + 1), :]) for a in range(PASSES)]
         page_t[3] = load_page(3)

from contextlib import ExitStack

import concourse.mybir as mybir
from concourse.masks import make_identity

K, H, N, T, S, T2 = 1024, 1024, 512, 2048, 1024, 2048
FLOPS = 2 * K * H * S + 2 * H * N * S + 2 * K * N * S

F32 = mybir.dt.float32
BF16 = mybir.dt.bfloat16
I32 = mybir.dt.int32
U32 = mybir.dt.uint32
U16 = mybir.dt.uint16
U8 = mybir.dt.uint8
FP8X4 = mybir.dt.float8_e4m3fn_x4
FP4X4 = mybir.dt.float4_e2m1fn_x4
ALU = mybir.AluOpType
ACT = mybir.ActivationFunctionType

P = 128
PACK = 4
PASS = P * PACK
PASSES = 2
BANK = 512
SLICES = PASSES * PACK
CHUNK = 256
ON_VECTOR = (0, 1, 4)


def tile_list_rotor_fault_scores_kernel(
    tc, tab_words, tab_scales, offs, w1, base, page0, wgs, offs2, wgt, offs3, w4_words, w4_scales, w2, b, out
):
    nc = tc.nc
    with ExitStack() as ctx:
        keep = ctx.enter_context(tc.tile_pool(name="keep", bufs=1))
        psum = ctx.enter_context(tc.psum_pool(name="psum", bufs=1))

        def bank_tile(index, shape, name):
            return psum.tile(shape, F32, name=name, tag="bank%d" % index)

        def load_list(src, name):
            tile = keep.tile([P, S // 16], U16, name=name)
            nc.sync.dma_start(tile[:], src)
            return tile

        def load_table_words(a):
            tile = keep.tile([P, T], I32, name="tab_w%d" % a)
            nc.sync.dma_start(tile[:], tab_words[a].rearrange("p t i -> p (t i)").bitcast(I32))
            return tile

        def load_weight(rows):
            raw = keep.tile([P, PACK, PASS], F32, name="raw", tag="raw", bufs=2)
            nc.sync.dma_start(raw[:], rows.rearrange("(p j) c -> p j c", j=PACK))
            return raw

        def bf_tile(width):
            return keep.tile([P, width], BF16, name="bf", tag="bf", bufs=4, align_bytes=64)

        def quantize(grouped, codes, scales):
            nc.vector.quantize_mx(out=codes.bitcast(FP8X4), scales=scales, in_=grouped[:])

        def quantize_weight(raw, name, dealt):
            t0, t1 = dealt or (0, PACK)
            grouped = bf_tile(PACK * P * (t1 - t0))
            if dealt:
                nc.scalar.copy(
                    out=grouped[:].rearrange("p (t m j) -> p m t j", t=t1 - t0, j=PACK),
                    in_=raw[:].rearrange("p j (m t) -> p m t j", t=PACK)[:, :, t0:t1, :],
                )
            else:
                nc.scalar.copy(
                    out=grouped[:].rearrange("p (c j) -> p c j", j=PACK),
                    in_=raw[:].rearrange("p j c -> p c j"),
                )
            codes = keep.tile([P, P * (t1 - t0)], U32, name=name + "_c", align_bytes=64)
            scales = keep.tile([P, P * (t1 - t0)], U8, name=name + "_s", align_bytes=64)
            quantize(grouped, codes[:], scales[:])
            return [(codes[:, P * i : P * (i + 1)], scales[:, P * i : P * (i + 1)]) for i in range(t1 - t0)]

        def slice_rows(src, s):
            rows = src[PASS * (s // PACK) : PASS * (s // PACK + 1), :]
            return rows.rearrange("(p t) j -> p t j", t=PACK)[:, s % PACK, :]

        def load_page(s):
            tile = keep.tile([P, T2], F32, name="page", tag="page", bufs=5)
            nc.sync.dma_start(tile[:], slice_rows(page0, s))
            return tile

        wgs_rows = wgs.rearrange("(q t) j -> q t j", t=PACK)

        wgs_t = [keep.tile([P, S], F32, name="wgs%d" % t) for t in range(PACK)]

        def load_wgs(t, cols=slice(0, S)):
            for quad in (0, 2, 1, 3):
                nc.sync.dma_start(wgs_t[t][32 * quad : 32 * quad + 32, cols], wgs_rows[:, t, cols])

        x_f = [keep.tile([P, PACK, S], F32, name="x_f%d" % g) for g in range(PASSES)]

        def x_plane(s):
            return x_f[s // PACK][:, s % PACK, :]

        def load_base(s):
            if s in ON_VECTOR:
                rows = keep.tile([P, S], F32, name="base", tag="base", bufs=2)[:]
            else:
                rows = x_plane(s - 2)
            nc.sync.dma_start(rows, slice_rows(base, s))
            return rows

        tab_s = keep.tile([P, T], U8, name="tab_s")
        nc.gpsimd.memset(tab_s[:].bitcast(I32), 0)
        for quad in range(4):
            nc.scalar.dma_start(
                tab_s[32 * quad : 32 * quad + 8, :].bitcast(I32), tab_scales[:, 4 * quad : 4 * quad + 4, :].bitcast(I32)
            )
        idx = load_list(offs, "idx")
        idx2 = load_list(offs2, "idx2")
        idx3 = load_list(offs3, "idx3")
        tab_w = [load_table_words(0)]
        raw = [load_weight(w1[0:PASS, 0:PASS])]
        tab_w.append(load_table_words(1))
        raw.append(load_weight(w1[PASS : 2 * PASS, 0:PASS]))
        halves = [slice(BANK * u, BANK * (u + 1)) for u in range(2)]
        base_t = {0: keep.tile([P, S], F32, name="base", tag="base", bufs=2)[:]}
        nc.sync.dma_start(base_t[0][:, halves[0]], slice_rows(base, 0)[:, halves[0]])
        page_t = {0: load_page(0)}
        load_wgs(0, halves[0])
        nc.sync.dma_start(base_t[0][:, halves[1]], slice_rows(base, 0)[:, halves[1]])
        load_wgs(0, halves[1])
        ident = keep.tile([P, P], F32, name="ident")
        make_identity(nc, ident[:])

        v_w = [keep.tile([P, S], U32, name="v_w%d" % a, align_bytes=64) for a in range(PASSES)]
        v_s = keep.tile([P, S], U8, name="v_s", align_bytes=64)
        nc.vector.tensor_copy(v_w[0][:], tab_w[0][:].bitcast(U32).indirect(idx[:]))
        nc.vector.tensor_copy(v_s[:], tab_s[:].indirect(idx[:]))
        w1_q = {(0, 0): quantize_weight(raw[0], "w1_00a", (0, 2))}
        nc.vector.tensor_copy(v_w[1][:], tab_w[1][:].bitcast(U32).indirect(idx[:]))
        w1_q[(0, 1)] = quantize_weight(raw[1], "w1_01a", (0, 2))

        def product_with_v(acc, weights, u):
            for a in range(PASSES):
                codes, scales = weights[a]
                nc.tensor.matmul_mx(
                    out=acc[:],
                    lhsT=codes.bitcast(FP8X4),
                    lhsT_scale=scales,
                    rhs=v_w[a][:, BANK * u : BANK * (u + 1)].bitcast(FP8X4),
                    rhs_scale=v_s[4 * a : P, BANK * u : BANK * (u + 1)],
                    start=(a == 0),
                    stop=(a == PASSES - 1),
                )

        def turn_blocks(acc, src, start, stop):
            for i in range(BANK // P):
                nc.tensor.matmul(
                    acc[:, P * i : P * (i + 1)],
                    lhsT=src[:, P * i : P * (i + 1)],
                    rhs=ident[:],
                    is_transpose=True,
                    start=start and i == 0,
                    stop=stop and i == BANK // P - 1,
                )

        def half_tile(name):
            return keep.tile([P, BANK], F32, name=name, tag=name, bufs=2)

        def make_h(s):
            g, t = divmod(s, PACK)
            h = keep.tile([P, S], F32, name="h", tag="h", bufs=3)
            if s == 5:
                a_t_both = keep.tile([P, S], F32, name="a_t_both", tag="raw", bufs=2)
                neg_a_both = keep.tile([P, S], F32, name="neg_a_both", tag="raw", bufs=2)
            for u in range(2):
                cols = slice(BANK * u, BANK * (u + 1))
                acc = bank_tile({0: 4, 1: 4, 4: 2}.get(s, 0) + u, [P, BANK], "acc_a")
                product_with_v(acc, [w1_q[(g, a)][t] for a in range(PASSES)], u)
                if s in ON_VECTOR:
                    nc.vector.tensor_tensor(h[:, cols], acc[:], base_t[s][:, cols], ALU.max)
                    continue
                if (s, u) == (SLICES - 1, 1):
                    neg_a = keep.tile([P, BANK], F32, name="neg_a_last", tag="hold_codes", align_bytes=64)[:]
                elif s == 5:
                    neg_a = neg_a_both[:, cols]
                else:
                    neg_a = half_tile("neg_a")[:]
                nc.scalar.activation(neg_a, acc[:], ACT.Copy, scale=-1.0)
                turned = bank_tile(2 + u, [P, BANK], "acc_t")
                turn_blocks(turned, neg_a, True, True)
                a_t = a_t_both[:, cols] if s == 5 else half_tile("a_t")[:]
                nc.scalar.activation(a_t, turned[:], ACT.Copy, scale=-1.0)
                diff = bank_tile(4 + u, [P, BANK], "acc_diff")
                turn_blocks(diff, neg_a, True, False)
                turn_blocks(diff, base_t[s][:, cols], False, True)
                if s == 6:
                    lift_t = keep.tile([P, BANK], F32, name="lift_hold", tag="hold%d" % u, align_bytes=64)[:]
                elif s in (3, 7):
                    lift_t = x_plane(s - 1)[:, cols]
                else:
                    lift_t = half_tile("lift_t")[:]
                nc.scalar.activation(lift_t, diff[:], ACT.Relu)
                back = bank_tile(6 + u, [P, BANK], "acc_h")
                turn_blocks(back, a_t, True, False)
                turn_blocks(back, lift_t, False, True)
                nc.scalar.copy(h[:, cols], back[:])
            return h

        def scatter(s, h, cols=slice(0, S)):
            places = idx2[:, cols.start // 16 : cols.stop // 16]
            nc.vector.tensor_tensor(page_t[s][:].indirect(places), h[:, cols], wgs_t[s % PACK][:, cols], ALU.mult)

        def gather(s, c0, c1):
            nc.vector.tensor_tensor(
                x_plane(s)[:, c0:c1], page_t[s][:].indirect(idx3[:, c0 // 16 : c1 // 16]), wgt_t[:, c0:c1], ALU.mult
            )

        def round_x(grouped, g, c0, c1):
            nc.scalar.copy(
                out=grouped[:].rearrange("p (c t) -> p c t", t=PACK),
                in_=x_f[g][:, :, c0:c1].rearrange("p t c -> p c t"),
            )
            return grouped

        h = make_h(0)
        for cols in halves:
            scatter(0, h, cols)
        base_t[1] = load_base(1)
        page_t[1] = load_page(1)
        load_wgs(1)
        h = make_h(1)
        for a in range(PASSES):
            w1_q[(0, a)].extend(quantize_weight(raw[a], "w1_0%db" % a, (2, PACK)))
        scatter(1, h)
        wgt_t = keep.tile([P, S], F32, name="wgt_t")
        nc.sync.dma_start(wgt_t[:], wgt)

        base_t[2] = load_base(2)
        load_wgs(2)
        h = make_h(2)
        gather(0, 0, S)
        for a in range(PASSES):
            w1_q[(1, a)] = quantize_weight(load_weight(w1[PASS * a : PASS * (a + 1), PASS : 2 * PASS]), "w1_1%d" % a, (0, PACK))
        page_t[2] = load_page(2)
        scatter(2, h)

        base_t[3] = load_base(3)
        load_wgs(3)
        base_t[4] = load_base(4)
        w2_raw = [load_weight(w2[PASS * a : PASS * (a + 1), :]) for a in range(PASSES)]
        page_t[3] = load_page(3)
        h = make_h(3)
        gather(1, 0, S)
        gather(2, 0, S)
        h_next = make_h(4)
        w2_q = [quantize_weight(w2_raw[a], "w2_%d" % a, None) for a in range(PASSES)]
        scatter(3, h)

        page_t[4] = load_page(4)
        base_t[5] = load_base(5)
        scatter(4, h_next)
        bias = keep.tile([P, N // P], F32, name="bias")
        with nc.allow_non_contiguous_dma(reason="one bias value a partition"):
            nc.sync.dma_start(bias[:], b.rearrange("(c p) -> p c", p=P))

        h = make_h(5)
        gather(3, 0, S)
        res = keep.tile([P, N // P, S], F32, name="res")
        for c in range(N // P):
            for u in range(2):
                acc = bank_tile(6 + u, [P, BANK], "acc_d")
                product_with_v(acc, [w2_q[a][c] for a in range(PASSES)], u)
                nc.scalar.activation(res[:, c, BANK * u : BANK * (u + 1)], acc[:], ACT.Identity, bias=bias[:, c : c + 1])

        page_t[5] = load_page(5)
        scatter(5, h)

        base_t[6] = load_base(6)
        page_t[6] = load_page(6)
        w4_w = keep.tile([P, PASSES, 2 * N], U8, name="w4_w", align_bytes=64)
        nc.sync.dma_start(w4_w[:].bitcast(I32), w4_words.rearrange("a p n -> p a n").bitcast(I32))
        w4_s = keep.tile([P, PASSES, N], U8, name="w4_s", align_bytes=64)
        nc.gpsimd.memset(w4_s[:].bitcast(I32), 0)
        for quad in range(4):
            nc.sync.dma_start(
                w4_s[32 * quad : 32 * quad + 4, :, :].bitcast(I32),
                w4_scales[:, 4 * quad : 4 * quad + 4, :].rearrange("a r n -> r a n").bitcast(I32),
            )
        h = make_h(6)
        gather(4, 0, S)
        scatter(6, h)

        x0_grouped = []
        for u in range(2):
            grouped = keep.tile([P, PACK * BANK], BF16, name="x0_bf", tag="hold%d" % u, align_bytes=64)
            x0_grouped.append(round_x(grouped, 0, BANK * u, BANK * (u + 1)))

        base_t[7] = load_base(7)
        page_t[7] = load_page(7)
        h = make_h(7)
        gather(5, 0, S)
        x_c = [keep.tile([P, S], U32, name="x_c0", tag="hold_codes", align_bytes=64)]
        x_c.append(keep.tile([P, S], U32, name="x_c1", align_bytes=64))
        x_s = [keep.tile([P, S], U8, name="x_s%d" % g, align_bytes=64) for g in range(PASSES)]
        for u in range(2):
            cols = slice(BANK * u, BANK * (u + 1))
            quantize(x0_grouped[u], x_c[0][:, cols], x_s[0][:, cols])
        gather(6, 0, S)
        scatter(7, h)

        def y_pass(acc, pair, g, cols, start, stop):
            for e in range(2):
                c = 2 * pair + e
                nc.tensor.matmul_mx(
                    out=acc[:, e, :],
                    lhsT=w4_w[:, g, 2 * P * c : 2 * P * (c + 1)].bitcast(FP4X4),
                    lhsT_scale=w4_s[:, g, P * c : P * (c + 1)],
                    rhs=x_c[g][:, cols].bitcast(FP8X4),
                    rhs_scale=x_s[g][:, cols],
                    start=start and e == 0,
                    stop=stop and e == 1,
                )

        chunks = [slice(c0, c0 + CHUNK) for c0 in range(0, S, CHUNK)]
        y_acc = {}
        for i, cols in enumerate(chunks):
            for pair in range(2):
                y_acc[(i, pair)] = bank_tile(2 * i + pair, [P, 2, CHUNK], "acc_y")
                y_pass(y_acc[(i, pair)], pair, 0, cols, True, False)
        for cols in chunks:
            gather(SLICES - 1, cols.start, cols.stop)
        out_rows = out.rearrange("(c p) m -> p c m", p=P)

        def finish_product(i):
            cols = chunks[i]
            quantize(round_x(bf_tile(PACK * CHUNK), 1, cols.start, cols.stop), x_c[1][:, cols], x_s[1][:, cols])
            for pair in range(2):
                y_pass(y_acc[(i, pair)], pair, 1, cols, False, True)

        def finish_scores(i):
            cols = chunks[i]
            for pair in range(2):
                for e in range(2):
                    c = 2 * pair + e
                    nc.vector.scalar_tensor_tensor(
                        res[:, c, cols], y_acc[(i, pair)][:, e, :], bias[:, c : c + 1], res[:, c, cols], ALU.add, ALU.max
                    )
                nc.sync.dma_start(out_rows[:, 2 * pair : 2 * pair + 2, cols], res[:, 2 * pair : 2 * pair + 2, cols])

        finish_product(0)
        for i in range(len(chunks)):
            if i + 1 < len(chunks):
                finish_product(i + 1)
            finish_scores(i)
